import numpy as np
import ml_dtypes


def mxq(x, axis, fmt="e4m3"):
    dtype, down = {"e4m3": (ml_dtypes.float8_e4m3fn, 7), "e5m2": (ml_dtypes.float8_e5m2, 14)}[fmt]
    v = np.moveaxis(np.asarray(x, np.float32).astype(ml_dtypes.bfloat16).astype(np.float64), axis, -1)
    blocks = v.reshape(v.shape[:-1] + (-1, 32))
    amax = np.abs(blocks).max(-1, keepdims=True)
    byte = np.maximum(np.where(amax > 0, np.frexp(amax)[1] - 1 + 127, 0) - down, 1)
    scale = np.exp2(byte - 127.0)
    codes = (blocks / scale).astype(np.float32).astype(dtype).astype(np.float64)
    return np.moveaxis((codes * scale).reshape(v.shape), -1, axis)


WIDE = False


def mx_kscale(k):
    if not WIDE:
        return np.ones(k)
    levels = np.array([10, -10, 5, -5, 0])
    if k % 512:
        return np.exp2(np.random.permutation(np.resize(levels, k // 32))).repeat(32)
    a = np.empty((k // 512, 16))
    for p in range(k // 512):
        a[p, :8] = np.random.permutation(np.resize(levels, 8))
        for g in range(8):
            far = levels[np.abs(levels - a[p, g]) >= 10]
            a[p, g + 8] = far[np.random.randint(len(far))]
    return np.exp2(a.ravel()).repeat(32)


def f64(x):
    return np.asarray(x).astype(np.float64)


def striped(idx):
    return np.tile(idx.reshape(-1, 16).T, (8, 1)).astype(np.uint16)


def unstriped(offs):
    return offs[:16].T.reshape(-1).astype(np.int64)


def striped8(idx):
    return np.concatenate([x.reshape(-1, 16).T for x in idx]).astype(np.uint16)


def runs(offs, k):
    lists = np.stack([offs[16 * r : 16 * r + 16].T.reshape(-1) for r in range(8)]).astype(np.int64)
    return lists[np.arange(k) % 512 // 64]


def pack_weight(w):
    k, n = w.shape
    w = f64(np.asarray(w, np.float32).astype(ml_dtypes.bfloat16)).reshape(k // 32, 32, n)
    amax = np.abs(w).max(1)
    byte = np.clip(np.where(amax > 0, np.frexp(amax)[1] - 1 + 127 - 7, 1), 1, 254)
    scaled = (w * np.exp2(127.0 - byte)[:, None, :]).reshape(k, n).astype(np.float32)
    words = np.ascontiguousarray(scaled.reshape(k // 512, 128, 4, n).transpose(0, 1, 3, 2)).astype(ml_dtypes.float8_e4m3fn).view(np.uint8)
    return words, np.ascontiguousarray(byte.astype(np.uint8).reshape(k // 512, 16, n))


def unpack_weight(words, scales):
    g, p, n, _ = words.shape
    vals = np.ascontiguousarray(words).view(ml_dtypes.float8_e4m3fn).astype(np.float64) * np.repeat(np.exp2(scales.astype(np.float64) - 127.0), 8, axis=1)[..., None]
    return vals.transpose(0, 1, 3, 2).reshape(g * 512, n)

def planes(y):
    n, m = y.shape
    v = y.astype(np.float32).astype(ml_dtypes.bfloat16).astype(np.float64).reshape(n // 32, 32, m)
    top = np.abs(v).max(1)
    byte = np.clip(np.where(top > 0, np.frexp(top)[1] - 1 + 127 - 7, 1), 1, 254)
    codes = (v * np.exp2(127.0 - byte)[:, None, :]).reshape(n, m).astype(np.float32).astype(ml_dtypes.float8_e4m3fn).view(np.uint8)
    words = codes.reshape(n // 512, 128, 4, m).transpose(0, 1, 3, 2)
    return np.ascontiguousarray(words), np.ascontiguousarray(byte.astype(np.uint8).reshape(n // 512, 16, m))


K, T, S, N, H = 512, 2048, 512, 512, 512


def setup_inputs():
    n = np.random.standard_normal
    s = mx_kscale(K)[:, None]
    u = mx_kscale(H)
    packed_xT = pack_weight(n((K, T)) * s)
    packed_w1 = pack_weight(n((K, H)) / np.sqrt(K) / s)
    packed_w2 = pack_weight(n((H, N)) / np.sqrt(2 * H) / u[:, None])
    packed_w3 = pack_weight(n((H, N)) / np.sqrt(2 * H) / u[:, None])
    return {
        "x_words": packed_xT[0],
        "x_scales": packed_xT[1],
        "w1_words": packed_w1[0],
        "w1_scales": packed_w1[1],
        "gn": (np.random.uniform(0.5, 1.5, (H, 1)) * u[:, None]).astype(np.float32),
        "gm": (np.random.uniform(0.5, 1.5, (H, 1)) * u[:, None]).astype(np.float32),
        "w2_words": packed_w2[0],
        "w2_scales": packed_w2[1],
        "w3_words": packed_w3[0],
        "w3_scales": packed_w3[1],
        "offs": striped(np.random.permutation(T)[:S]),
        "n1": striped8(np.stack([np.random.permutation(S) for _ in range(8)])),
        "n2": striped8(np.stack([np.random.permutation(S) for _ in range(8)])),
        "n3": striped8(np.stack([np.random.permutation(S) for _ in range(8)])),
        "n4": striped8(np.stack([np.random.permutation(S) for _ in range(8)])),
        "n5": striped8(np.stack([np.random.permutation(S) for _ in range(8)])),
    }


def reference(x_words, x_scales, w1_words, w1_scales, gn, gm, w2_words, w2_scales, w3_words, w3_scales, offs, n1, n2, n3, n4, n5):
    xq = unpack_weight(x_words, x_scales)[:, unstriped(offs)]
    y = unpack_weight(w1_words, w1_scales).T @ xq
    st = y + y[np.arange(H)[:, None], runs(n1, H)]
    z = f64(gn) * (st * (np.tanh(st[np.arange(H)[:, None], runs(n2, H)])))
    pa = y[np.arange(H)[:, None], runs(n3, H)]
    z2 = f64(gm) * ((2.0 * (y * pa)) / ((y) ** 2 + (pa) ** 2 + 0.5))
    h = unpack_weight(w2_words, w2_scales).T @ mxq(z, 0, "e4m3") + unpack_weight(w3_words, w3_scales).T @ mxq(z2, 0, "e4m3")
    out_0 = h - (np.minimum(h[np.arange(N)[:, None], runs(n4, N)], h[np.arange(N)[:, None], runs(n5, N)]))
    return (out_0,) + planes(out_0)

@@ -1,0 +1,248 @@
+from contextlib import ExitStack
+
+import concourse.mybir as mybir
+from concourse.masks import make_identity
+
+K, T, S, N, H = 512, 2048, 512, 512, 512
+FLOPS = 3 * 2 * 512 * 512 * 512
+
+F32 = mybir.dt.float32
+BF16 = mybir.dt.bfloat16
+I32 = mybir.dt.int32
+U32 = mybir.dt.uint32
+U16 = mybir.dt.uint16
+U8 = mybir.dt.uint8
+FP8X4 = mybir.dt.float8_e4m3fn_x4
+ALU = mybir.AluOpType
+ACT = mybir.ActivationFunctionType
+
+P = 128
+PACK = 4
+CW = 128
+LAST = [(0, 128), (128, 256), (384, 128)]
+
+
+def tile_picked_joinhoppharmunder_none_po_kernel(
+    tc, x_words, x_scales, w1_words, w1_scales, gn, gm, w2_words, w2_scales, w3_words, w3_scales,
+    offs, n1, n2, n3, n4, n5, out_0, out_1, out_2,
+):
+    nc = tc.nc
+    with ExitStack() as ctx:
+        keep = ctx.enter_context(tc.tile_pool(name="keep", bufs=1))
+        psum = ctx.enter_context(tc.psum_pool(name="psum", bufs=1))
+
+        def sb(name, shape, dtype):
+            return keep.tile(shape, dtype, name=name, align_bytes=64)
+
+        def load_list(name, src):
+            lst = keep.tile([P, S // 16], U16, name=name)
+            nc.sync.dma_start(lst[:], src)
+            return lst
+
+        def entries(lst, first, count):
+            return lst[:, first // 16 : (first + count) // 16]
+
+        def load_words(name, src, cols):
+            words = sb(name, [P, cols], I32)
+            nc.sync.dma_start(words[:], src[0].rearrange("p n t -> p (n t)").bitcast(I32))
+            return words
+
+        def load_scale_rows(plane, src, row0):
+            for q in range(4):
+                nc.sync.dma_start(
+                    plane[32 * q + row0 : 32 * q + row0 + 4, :].bitcast(I32),
+                    src[0, 4 * q : 4 * q + 4, :].bitcast(I32),
+                )
+
+        def load_scale_rows_repeated(plane, src):
+            for q in range(4):
+                rows = src[0, 4 * q : 4 * q + 4, :].bitcast(I32)
+                nc.sync.dma_start(
+                    plane[32 * q : 32 * q + 32, :].bitcast(I32), rows.unsqueeze(0).to_broadcast([8, 4, rows.shape[1]])
+                )
+
+        def deal(dst, src):
+            nc.vector.tensor_copy(
+                dst.rearrange("p (t m) -> p t m", t=PACK), src.rearrange("p (m t) -> p t m", t=PACK)
+            )
+
+        xs_all = sb("xs_all", [P, T], U8)
+        w1s_raw = sb("w1s_raw", [P, H], U8)
+        w23s_raw = sb("w23s_raw", [P, N], U8)
+        nc.vector.memset(w23s_raw[:].bitcast(I32), 0)
+        tiny = sb("tiny", [P, 1], F32)
+        nc.vector.memset(tiny[:], 2.0**-60)
+        warm = sb("warm", [P, 1], F32)
+        nc.scalar.activation(warm[:], tiny[:], ACT.Ln)
+
+        l_offs = load_list("l_offs", offs)
+        load_scale_rows_repeated(xs_all, x_scales)
+        xw_all = load_words("xw_all", x_words, T)
+        w1_raw = load_words("w1_raw", w1_words, H)
+        load_scale_rows_repeated(w1s_raw, w1_scales)
+        l3 = load_list("l3", n3)
+        w3_raw = load_words("w3_raw", w3_words, N)
+        w2_raw = load_words("w2_raw", w2_words, N)
+        l1 = load_list("l1", n1)
+        l2 = load_list("l2", n2)
+        gn_t = sb("gn_t", [P, PACK], F32)
+        nc.sync.dma_start(gn_t[:], gn.rearrange("(p t) o -> p (t o)", t=PACK))
+        gm_t = sb("gm_t", [P, PACK], F32)
+        nc.sync.dma_start(gm_t[:], gm.rearrange("(p t) o -> p (t o)", t=PACK))
+        load_scale_rows(w23s_raw, w2_scales, 0)
+        load_scale_rows(w23s_raw, w3_scales, 4)
+        l4 = load_list("l4", n4)
+        l5 = load_list("l5", n5)
+
+        ident = sb("ident", [P, P], F32)
+        make_identity(nc, ident[:])
+        gn2 = sb("gn2", [P, PACK], F32)
+        nc.gpsimd.tensor_scalar(gn2[:], gn_t[:], 2.0, 0.0, ALU.mult, ALU.add)
+        gm4 = sb("gm4", [P, PACK], F32)
+        nc.gpsimd.tensor_scalar(gm4[:], gm_t[:], 4.0, 0.0, ALU.mult, ALU.add)
+
+        xs = sb("xs", [P, S], U8)
+        nc.vector.tensor_copy(xs[:], xs_all[:].indirect(l_offs[:]))
+        xw = sb("xw", [P, S], U32)
+        half = S // 2
+        for u in range(2):
+            nc.vector.tensor_copy(
+                xw[:, u * half : (u + 1) * half],
+                xw_all[:].bitcast(U32).indirect(entries(l_offs, u * half, half)),
+            )
+        w1s = sb("w1s", [P, H], U8)
+        deal(w1s[:], w1s_raw[:])
+        w1 = sb("w1", [P, H], I32)
+        deal(w1[:], w1_raw[:])
+
+        y = [sb("y%d" % t, [P, S], F32) for t in range(PACK)]
+        y_again = sb("y_again", [P, PACK, S], F32)
+        sq_y = sb("sq_y", [P, PACK, S], F32)
+        for t in range(PACK):
+            acc = psum.tile([P, S], F32, name="y_acc%d" % t, tag="a%d" % t)
+            rows = slice(t * P, (t + 1) * P)
+            nc.tensor.matmul_mx(
+                acc[:], lhsT=w1[:, rows].bitcast(FP8X4), lhsT_scale=w1s[:, rows],
+                rhs=xw[:].bitcast(FP8X4), rhs_scale=xs[:], start=True, stop=True,
+            )
+            nc.scalar.copy(y[t][:], acc[:])
+            nc.sync.dma_start(y_again[:, t, :], y[t][:])
+            nc.gpsimd.tensor_tensor(sq_y[:, t, :], y[t][:], y[t][:], ALU.mult)
+
+        w23s = sb("w23s", [P, N], U8)
+        w2 = sb("w2", [P, N], I32)
+        w3 = sb("w3", [P, N], I32)
+        deal(w3[:], w3_raw[:])
+        deal(w2[:], w2_raw[:])
+
+        pa = sb("pa", [P, PACK, S], F32)
+        sq_pa = sb("sq_pa", [P, PACK, S], F32)
+        work = sb("work", [P, PACK, S], F32)
+        for t in range(PACK):
+            for u in range(2):
+                nc.vector.tensor_copy(
+                    pa[:, t, u * half : (u + 1) * half], y[t][:].indirect(entries(l3, u * half, half))
+                )
+            nc.scalar.activation(sq_pa[:, t, :], pa[:, t, :], ACT.Square)
+            q_acc = psum.tile([P, S], F32, name="q_acc%d" % t, tag="b%d" % t)
+            for c in range(S // P):
+                cols = slice(c * P, (c + 1) * P)
+                nc.tensor.matmul(q_acc[:, cols], sq_y[:, t, cols], ident[:], start=True, stop=False, is_transpose=True)
+                nc.tensor.matmul(q_acc[:, cols], sq_pa[:, t, cols], ident[:], start=False, stop=True, is_transpose=True)
+            nc.scalar.activation(work[:, t, :], q_acc[:], ACT.Ln, bias=tiny[:], scale=2.0)
+
+        st = [sb("st%d" % t, [P, S], F32) for t in range(PACK)]
+        st_again = sb("st_again", [P, PACK, S], F32)
+        for t in range(PACK):
+            for u in range(2):
+                cols = slice(u * half, (u + 1) * half)
+                nc.vector.tensor_tensor(
+                    st[t][:, cols], y[t][:].indirect(entries(l1, u * half, half)), y_again[:, t, cols], ALU.add
+                )
+            nc.sync.dma_start(st_again[:, t, :], st[t][:])
+        deal(w23s[:], w23s_raw[:])
+        num = sb("num", [P, PACK, S], F32)
+        for t in range(PACK):
+            nc.vector.scalar_tensor_tensor(
+                num[:, t, :], pa[:, t, :], gm4[:, t : t + 1], y[t][:], ALU.mult, ALU.mult
+            )
+
+        h_acc = [psum.tile([P, S], F32, name="h_acc%d" % t, tag="b%d" % t) for t in range(PACK)]
+        neg_h = [sb("neg_h%d" % t, [P, S], F32) for t in range(PACK)]
+        neg_h_again = sb("neg_h_again", [P, PACK, S], F32)
+        tanh_g = sb("tanh_g", [P, PACK, S], F32)
+
+        def woven(ap):
+            return ap.rearrange("p t (c i) -> p c t i", i=2)
+
+        for c in range(S // CW):
+            cols = slice(c * CW, (c + 1) * CW)
+            recip_t = sb("recip_t%d" % c, [P, PACK, P], F32)
+            nc.scalar.activation(recip_t[:], work[:, :, cols], ACT.Sigmoid, scale=-1.0)
+            recip = psum.tile([P, PACK, P], F32, name="recip%d" % c, tag="a%d" % c)
+            for t in range(PACK):
+                nc.tensor.transpose(recip[:, t, :], recip_t[:, t, :], ident[:])
+            for t in range(PACK):
+                nc.scalar.activation(
+                    work[:, t, cols], st[t][:].indirect(entries(l2, c * CW, CW)), ACT.Sigmoid, scale=2.0
+                )
+            zz = sb("zz%d" % c, [P, 2, CW, PACK], BF16)
+            nc.vector.tensor_tensor(
+                zz[:, 0].rearrange("p (c i) t -> p c t i", i=2), woven(num[:, :, cols]), woven(recip[:]), ALU.mult
+            )
+            for t in range(PACK):
+                nc.vector.tensor_scalar(
+                    tanh_g[:, t, cols], work[:, t, cols], 0.5, gn2[:, t : t + 1], ALU.subtract, ALU.mult
+                )
+            nc.vector.tensor_tensor(
+                zz[:, 1].rearrange("p (c i) t -> p c t i", i=2),
+                woven(tanh_g[:, :, cols]), woven(st_again[:, :, cols]), ALU.mult,
+            )
+            codes = sb("codes%d" % c, [P, 2 * CW], U32)
+            scales = sb("scales%d" % c, [P, 2 * CW], U8)
+            nc.vector.quantize_mx(codes[:].bitcast(FP8X4), scales[:], zz[:].rearrange("p a c t -> p (a c t)"))
+            for t in range(PACK):
+                rows = slice(t * P, (t + 1) * P)
+                nc.tensor.matmul_mx(
+                    h_acc[t][:, cols], lhsT=w3[:, rows].bitcast(FP8X4), lhsT_scale=w23s[4:, rows],
+                    rhs=codes[:, 0:CW].bitcast(FP8X4), rhs_scale=scales[:, 0:CW], start=True, stop=False,
+                )
+                nc.tensor.matmul_mx(
+                    h_acc[t][:, cols], lhsT=w2[:, rows].bitcast(FP8X4), lhsT_scale=w23s[:, rows],
+                    rhs=codes[:, CW:].bitcast(FP8X4), rhs_scale=scales[:, CW:], start=False, stop=True,
+                )
+                nc.scalar.activation(neg_h[t][:, cols], h_acc[t][:, cols], ACT.Copy, scale=-1.0)
+                for first, count in LAST:
+                    if first + count == (c + 1) * CW:
+                        nc.sync.dma_start(neg_h_again[:, t, first : first + count], neg_h[t][:, first : first + count])
+
+        out_rows = out_0.rearrange("(p t) j -> p t j", t=PACK)
+        out_words = out_1[0].rearrange("p n t -> p (n t)").bitcast(I32)
+        o_codes = sb("o_codes", [P, S], U32)
+        o_scales = sb("o_scales", [P, S], U8)
+        for first, count in LAST:
+            cols = slice(first, first + count)
+            less4 = sb("less4_%d" % first, [P, PACK, count], F32)
+            less5 = sb("less5_%d" % first, [P, PACK, count], F32)
+            for t in range(PACK):
+                for dst, lst in ((less4, l4), (less5, l5)):
+                    nc.vector.tensor_tensor(
+                        dst[:, t, :], neg_h[t][:].indirect(entries(lst, first, count)),
+                        neg_h_again[:, t, cols], ALU.subtract,
+                    )
+            res = sb("res%d" % first, [P, PACK, count], F32)
+            nc.vector.tensor_tensor(res[:], less4[:], less5[:], ALU.max)
+            nc.sync.dma_start(out_rows[:, :, cols], res[:])
+            rounded = sb("rounded%d" % first, [P, count, PACK], BF16)
+            copy = nc.vector.tensor_copy if first + count == S else nc.scalar.copy
+            copy(
+                rounded[:].rearrange("p (c i) t -> p c t i", i=4),
+                res[:].rearrange("p t (c i) -> p c t i", i=4),
+            )
+            nc.vector.quantize_mx(
+                o_codes[:, cols].bitcast(FP8X4), o_scales[:, cols], rounded[:].rearrange("p c t -> p (c t)")
+            )
+            nc.sync.dma_start(out_words[:, cols], o_codes[:, cols].bitcast(I32))
+        for q in range(4):
+            queue = nc.sync if q % 2 else nc.scalar
+            queue.dma_start(out_2[0, 4 * q : 4 * q + 4, :].bitcast(I32), o_scales[32 * q : 32 * q + 4, :].bitcast(I32))

@@ -61,9 +61,10 @@ def tile_picked_joinhoppharmunder_none_po_kernel(
                     plane[32 * q : 32 * q + 32, :].bitcast(I32), rows.unsqueeze(0).to_broadcast([8, 4, rows.shape[1]])
                 )
 
-        def deal(dst, src):
+        def deal(dst, src, first=0, count=PACK):
             nc.vector.tensor_copy(
-                dst.rearrange("p (t m) -> p t m", t=PACK), src.rearrange("p (m t) -> p t m", t=PACK)
+                dst.rearrange("p (t m) -> p t m", t=PACK)[:, first : first + count, :],
+                src.rearrange("p (m t) -> p t m", t=PACK)[:, first : first + count, :],
             )
 
         xs_all = sb("xs_all", [P, T], U8)
@@ -81,14 +82,14 @@ def tile_picked_joinhoppharmunder_none_po_kernel(
         w1_raw = load_words("w1_raw", w1_words, H)
         load_scale_rows_repeated(w1s_raw, w1_scales)
         l3 = load_list("l3", n3)
-        w3_raw = load_words("w3_raw", w3_words, N)
-        w2_raw = load_words("w2_raw", w2_words, N)
-        l1 = load_list("l1", n1)
-        l2 = load_list("l2", n2)
         gn_t = sb("gn_t", [P, PACK], F32)
         nc.sync.dma_start(gn_t[:], gn.rearrange("(p t) o -> p (t o)", t=PACK))
         gm_t = sb("gm_t", [P, PACK], F32)
         nc.sync.dma_start(gm_t[:], gm.rearrange("(p t) o -> p (t o)", t=PACK))
+        l1 = load_list("l1", n1)
+        l2 = load_list("l2", n2)
+        w3_raw = load_words("w3_raw", w3_words, N)
+        w2_raw = load_words("w2_raw", w2_words, N)
         load_scale_rows(w23s_raw, w2_scales, 0)
         load_scale_rows(w23s_raw, w3_scales, 4)
         l4 = load_list("l4", n4)
@@ -97,43 +98,49 @@ def tile_picked_joinhoppharmunder_none_po_kernel(
         ident = sb("ident", [P, P], F32)
         make_identity(nc, ident[:])
         gn2 = sb("gn2", [P, PACK], F32)
-        nc.gpsimd.tensor_scalar(gn2[:], gn_t[:], 2.0, 0.0, ALU.mult, ALU.add)
+        nc.scalar.activation(gn2[:], gn_t[:], ACT.Copy, scale=2.0)
         gm4 = sb("gm4", [P, PACK], F32)
-        nc.gpsimd.tensor_scalar(gm4[:], gm_t[:], 4.0, 0.0, ALU.mult, ALU.add)
+        nc.scalar.activation(gm4[:], gm_t[:], ACT.Copy, scale=4.0)
 
         xs = sb("xs", [P, S], U8)
         nc.vector.tensor_copy(xs[:], xs_all[:].indirect(l_offs[:]))
         xw = sb("xw", [P, S], U32)
-        half = S // 2
-        for u in range(2):
-            nc.vector.tensor_copy(
-                xw[:, u * half : (u + 1) * half],
-                xw_all[:].bitcast(U32).indirect(entries(l_offs, u * half, half)),
-            )
         w1s = sb("w1s", [P, H], U8)
-        deal(w1s[:], w1s_raw[:])
         w1 = sb("w1", [P, H], I32)
-        deal(w1[:], w1_raw[:])
-
+        half = S // 2
         y = [sb("y%d" % t, [P, S], F32) for t in range(PACK)]
         y_again = sb("y_again", [P, PACK, S], F32)
-        sq_y = sb("sq_y", [P, PACK, S], F32)
-        for t in range(PACK):
-            acc = psum.tile([P, S], F32, name="y_acc%d" % t, tag="a%d" % t)
+
+        def project(acc, t, cols):
             rows = slice(t * P, (t + 1) * P)
             nc.tensor.matmul_mx(
-                acc[:], lhsT=w1[:, rows].bitcast(FP8X4), lhsT_scale=w1s[:, rows],
-                rhs=xw[:].bitcast(FP8X4), rhs_scale=xs[:], start=True, stop=True,
+                acc, lhsT=w1[:, rows].bitcast(FP8X4), lhsT_scale=w1s[:, rows],
+                rhs=xw[:, cols].bitcast(FP8X4), rhs_scale=xs[:, cols], start=True, stop=True,
             )
+
+        nc.vector.tensor_copy(xw[:, :half], xw_all[:].bitcast(U32).indirect(entries(l_offs, 0, half)))
+        deal(w1[:], w1_raw[:], 0, 1)
+        deal(w1s[:], w1s_raw[:], 0, 1)
+        early = psum.tile([P, half], F32, name="y_early", tag="b0")
+        project(early[:], 0, slice(0, half))
+        nc.scalar.copy(y[0][:, :half], early[:])
+        nc.vector.tensor_copy(xw[:, half:], xw_all[:].bitcast(U32).indirect(entries(l_offs, half, half)))
+        late = psum.tile([P, half], F32, name="y_late", tag="a0")
+        project(late[:], 0, slice(half, S))
+        deal(w1[:], w1_raw[:], 1, 3)
+        deal(w1s[:], w1s_raw[:], 1, 3)
+        nc.vector.tensor_copy(y[0][:, half:], late[:])
+        nc.sync.dma_start(y_again[:, 0, :], y[0][:])
+        for t in range(1, PACK):
+            acc = psum.tile([P, S], F32, name="y_acc%d" % t, tag="a%d" % t)
+            project(acc[:], t, slice(0, S))
             nc.scalar.copy(y[t][:], acc[:])
             nc.sync.dma_start(y_again[:, t, :], y[t][:])
-            nc.gpsimd.tensor_tensor(sq_y[:, t, :], y[t][:], y[t][:], ALU.mult)
 
         w23s = sb("w23s", [P, N], U8)
         w2 = sb("w2", [P, N], I32)
         w3 = sb("w3", [P, N], I32)
-        deal(w3[:], w3_raw[:])
-        deal(w2[:], w2_raw[:])
+        sq_y = sb("sq_y", [P, PACK, S], F32)
 
         pa = sb("pa", [P, PACK, S], F32)
         sq_pa = sb("sq_pa", [P, PACK, S], F32)
@@ -143,12 +150,16 @@ def tile_picked_joinhoppharmunder_none_po_kernel(
                 nc.vector.tensor_copy(
                     pa[:, t, u * half : (u + 1) * half], y[t][:].indirect(entries(l3, u * half, half))
                 )
+            nc.scalar.activation(sq_y[:, t, :], y[t][:], ACT.Square)
             nc.scalar.activation(sq_pa[:, t, :], pa[:, t, :], ACT.Square)
             q_acc = psum.tile([P, S], F32, name="q_acc%d" % t, tag="b%d" % t)
-            for c in range(S // P):
-                cols = slice(c * P, (c + 1) * P)
-                nc.tensor.matmul(q_acc[:, cols], sq_y[:, t, cols], ident[:], start=True, stop=False, is_transpose=True)
-                nc.tensor.matmul(q_acc[:, cols], sq_pa[:, t, cols], ident[:], start=False, stop=True, is_transpose=True)
+            for k, squares in enumerate((sq_y, sq_pa)):
+                for c in range(S // P):
+                    cols = slice(c * P, (c + 1) * P)
+                    nc.tensor.matmul(
+                        q_acc[:, cols], squares[:, t, cols], ident[:],
+                        start=(k == 0 and c == 0), stop=(k == 1 and c == S // P - 1), is_transpose=True,
+                    )
             nc.scalar.activation(work[:, t, :], q_acc[:], ACT.Ln, bias=tiny[:], scale=2.0)
 
         st = [sb("st%d" % t, [P, S], F32) for t in range(PACK)]
@@ -160,6 +171,8 @@ def tile_picked_joinhoppharmunder_none_po_kernel(
                     st[t][:, cols], y[t][:].indirect(entries(l1, u * half, half)), y_again[:, t, cols], ALU.add
                 )
             nc.sync.dma_start(st_again[:, t, :], st[t][:])
+        deal(w3[:], w3_raw[:])
+        deal(w2[:], w2_raw[:])
         deal(w23s[:], w23s_raw[:])
         num = sb("num", [P, PACK, S], F32)
         for t in range(PACK):
@@ -211,7 +224,10 @@ def tile_picked_joinhoppharmunder_none_po_kernel(
                     h_acc[t][:, cols], lhsT=w2[:, rows].bitcast(FP8X4), lhsT_scale=w23s[:, rows],
                     rhs=codes[:, CW:].bitcast(FP8X4), rhs_scale=scales[:, CW:], start=False, stop=True,
                 )
-                nc.scalar.activation(neg_h[t][:, cols], h_acc[t][:, cols], ACT.Copy, scale=-1.0)
+                if c == S // CW - 1 and t % 2 == 0:
+                    nc.vector.tensor_scalar(neg_h[t][:, cols], h_acc[t][:, cols], -1.0, None, ALU.mult)
+                else:
+                    nc.scalar.activation(neg_h[t][:, cols], h_acc[t][:, cols], ACT.Copy, scale=-1.0)
                 for first, count in LAST:
                     if first + count == (c + 1) * CW:
                         nc.sync.dma_start(neg_h_again[:, t, first : first + count], neg_h[t][:, first : first + count])
@@ -224,14 +240,20 @@ def tile_picked_joinhoppharmunder_none_po_kernel(
             cols = slice(first, first + count)
             less4 = sb("less4_%d" % first, [P, PACK, count], F32)
             less5 = sb("less5_%d" % first, [P, PACK, count], F32)
+            res = sb("res%d" % first, [P, PACK, count], F32)
+            final = first + count == S
             for t in range(PACK):
                 for dst, lst in ((less4, l4), (less5, l5)):
                     nc.vector.tensor_tensor(
                         dst[:, t, :], neg_h[t][:].indirect(entries(lst, first, count)),
                         neg_h_again[:, t, cols], ALU.subtract,
                     )
-            res = sb("res%d" % first, [P, PACK, count], F32)
-            nc.vector.tensor_tensor(res[:], less4[:], less5[:], ALU.max)
+                if final and t > 0:
+                    nc.vector.tensor_tensor(res[:, t - 1, :], less4[:, t - 1, :], less5[:, t - 1, :], ALU.max)
+            if final:
+                nc.vector.tensor_tensor(res[:, PACK - 1, :], less4[:, PACK - 1, :], less5[:, PACK - 1, :], ALU.max)
+            else:
+                nc.vector.tensor_tensor(res[:], less4[:], less5[:], ALU.max)
             nc.sync.dma_start(out_rows[:, :, cols], res[:])
             rounded = sb("rounded%d" % first, [P, count, PACK], BF16)
             copy = nc.vector.tensor_copy if first + count == S else nc.scalar.copy

@@ -18,8 +18,8 @@ ACT = mybir.ActivationFunctionType
 
 P = 128
 PACK = 4
-CW = 128
-LAST = [(0, 128), (128, 256), (384, 128)]
+CHUNKS = [(0, 256), (256, 128), (384, 128)]
+RESULT_CHUNKS = [(0, 128), (128, 256), (384, 128)]
 
 
 def tile_picked_joinhoppharmunder_none_po_kernel(
@@ -29,6 +29,7 @@ def tile_picked_joinhoppharmunder_none_po_kernel(
     nc = tc.nc
     with ExitStack() as ctx:
         keep = ctx.enter_context(tc.tile_pool(name="keep", bufs=1))
+        shared = ctx.enter_context(tc.tile_pool(name="shared", bufs=1))
         psum = ctx.enter_context(tc.psum_pool(name="psum", bufs=1))
 
         def sb(name, shape, dtype):
@@ -61,10 +62,10 @@ def tile_picked_joinhoppharmunder_none_po_kernel(
                     plane[32 * q : 32 * q + 32, :].bitcast(I32), rows.unsqueeze(0).to_broadcast([8, 4, rows.shape[1]])
                 )
 
-        def deal(dst, src, first=0, count=PACK):
+        def deal(dst, src, run, first=0, count=PACK):
             nc.vector.tensor_copy(
-                dst.rearrange("p (t m) -> p t m", t=PACK)[:, first : first + count, :],
-                src.rearrange("p (m t) -> p t m", t=PACK)[:, first : first + count, :],
+                dst.rearrange("p (t b i) -> p b t i", t=PACK, i=run)[:, :, first : first + count, :],
+                src.rearrange("p (b i t) -> p b t i", t=PACK, i=run)[:, :, first : first + count, :],
             )
 
         xs_all = sb("xs_all", [P, T], U8)
@@ -73,14 +74,12 @@ def tile_picked_joinhoppharmunder_none_po_kernel(
         nc.vector.memset(w23s_raw[:].bitcast(I32), 0)
         tiny = sb("tiny", [P, 1], F32)
         nc.vector.memset(tiny[:], 2.0**-60)
-        warm = sb("warm", [P, 1], F32)
-        nc.scalar.activation(warm[:], tiny[:], ACT.Ln)
 
         l_offs = load_list("l_offs", offs)
         load_scale_rows_repeated(xs_all, x_scales)
         xw_all = load_words("xw_all", x_words, T)
-        w1_raw = load_words("w1_raw", w1_words, H)
         load_scale_rows_repeated(w1s_raw, w1_scales)
+        w1_raw = load_words("w1_raw", w1_words, H)
         l3 = load_list("l3", n3)
         gn_t = sb("gn_t", [P, PACK], F32)
         nc.sync.dma_start(gn_t[:], gn.rearrange("(p t) o -> p (t o)", t=PACK))
@@ -99,8 +98,6 @@ def tile_picked_joinhoppharmunder_none_po_kernel(
         make_identity(nc, ident[:])
         gn2 = sb("gn2", [P, PACK], F32)
         nc.scalar.activation(gn2[:], gn_t[:], ACT.Copy, scale=2.0)
-        gm4 = sb("gm4", [P, PACK], F32)
-        nc.scalar.activation(gm4[:], gm_t[:], ACT.Copy, scale=4.0)
 
         xs = sb("xs", [P, S], U8)
         nc.vector.tensor_copy(xs[:], xs_all[:].indirect(l_offs[:]))
@@ -109,7 +106,7 @@ def tile_picked_joinhoppharmunder_none_po_kernel(
         w1 = sb("w1", [P, H], I32)
         half = S // 2
         y = [sb("y%d" % t, [P, S], F32) for t in range(PACK)]
-        y_again = sb("y_again", [P, PACK, S], F32)
+        y_again = shared.tile([P, PACK, S], F32, name="y_again", offset=0, align_bytes=64)
 
         def project(acc, t, cols):
             rows = slice(t * P, (t + 1) * P)
@@ -119,16 +116,15 @@ def tile_picked_joinhoppharmunder_none_po_kernel(
             )
 
         nc.vector.tensor_copy(xw[:, :half], xw_all[:].bitcast(U32).indirect(entries(l_offs, 0, half)))
-        deal(w1[:], w1_raw[:], 0, 1)
-        deal(w1s[:], w1s_raw[:], 0, 1)
+        deal(w1s[:], w1s_raw[:], 16)
+        deal(w1[:], w1_raw[:], 4, 0, 1)
         early = psum.tile([P, half], F32, name="y_early", tag="b0")
         project(early[:], 0, slice(0, half))
         nc.scalar.copy(y[0][:, :half], early[:])
         nc.vector.tensor_copy(xw[:, half:], xw_all[:].bitcast(U32).indirect(entries(l_offs, half, half)))
         late = psum.tile([P, half], F32, name="y_late", tag="a0")
         project(late[:], 0, slice(half, S))
-        deal(w1[:], w1_raw[:], 1, 3)
-        deal(w1s[:], w1s_raw[:], 1, 3)
+        deal(w1[:], w1_raw[:], 4, 1, 3)
         nc.vector.tensor_copy(y[0][:, half:], late[:])
         nc.sync.dma_start(y_again[:, 0, :], y[0][:])
         for t in range(1, PACK):
@@ -137,9 +133,6 @@ def tile_picked_joinhoppharmunder_none_po_kernel(
             nc.scalar.copy(y[t][:], acc[:])
             nc.sync.dma_start(y_again[:, t, :], y[t][:])
 
-        w23s = sb("w23s", [P, N], U8)
-        w2 = sb("w2", [P, N], I32)
-        w3 = sb("w3", [P, N], I32)
         sq_y = sb("sq_y", [P, PACK, S], F32)
 
         pa = sb("pa", [P, PACK, S], F32)
@@ -171,14 +164,19 @@ def tile_picked_joinhoppharmunder_none_po_kernel(
                     st[t][:, cols], y[t][:].indirect(entries(l1, u * half, half)), y_again[:, t, cols], ALU.add
                 )
             nc.sync.dma_start(st_again[:, t, :], st[t][:])
-        deal(w3[:], w3_raw[:])
-        deal(w2[:], w2_raw[:])
-        deal(w23s[:], w23s_raw[:])
+        gm4 = shared.tile([P, PACK], F32, name="gm4", offset=0, align_bytes=64)
+        w23s = shared.tile([P, N], U8, name="w23s", offset=1024, align_bytes=64)
+        w2 = shared.tile([P, N], I32, name="w2", offset=2048, align_bytes=64)
+        w3 = shared.tile([P, N], I32, name="w3", offset=4096, align_bytes=64)
+        nc.vector.tensor_scalar(gm4[:], gm_t[:], 4.0, None, ALU.mult)
+        deal(w3[:], w3_raw[:], 4)
         num = sb("num", [P, PACK, S], F32)
         for t in range(PACK):
             nc.vector.scalar_tensor_tensor(
                 num[:, t, :], pa[:, t, :], gm4[:, t : t + 1], y[t][:], ALU.mult, ALU.mult
             )
+        deal(w2[:], w2_raw[:], 4)
+        deal(w23s[:], w23s_raw[:], 16)
 
         h_acc = [psum.tile([P, S], F32, name="h_acc%d" % t, tag="b%d" % t) for t in range(PACK)]
         neg_h = [sb("neg_h%d" % t, [P, S], F32) for t in range(PACK)]
@@ -186,57 +184,64 @@ def tile_picked_joinhoppharmunder_none_po_kernel(
         tanh_g = sb("tanh_g", [P, PACK, S], F32)
 
         def woven(ap):
-            return ap.rearrange("p t (c i) -> p c t i", i=2)
+            return ap.rearrange("p t (c i) -> p c t i", i=4)
 
-        for c in range(S // CW):
-            cols = slice(c * CW, (c + 1) * CW)
-            recip_t = sb("recip_t%d" % c, [P, PACK, P], F32)
-            nc.scalar.activation(recip_t[:], work[:, :, cols], ACT.Sigmoid, scale=-1.0)
-            recip = psum.tile([P, PACK, P], F32, name="recip%d" % c, tag="a%d" % c)
-            for t in range(PACK):
-                nc.tensor.transpose(recip[:, t, :], recip_t[:, t, :], ident[:])
+        recip = {}
+        for first, count in CHUNKS:
+            for c in range(first // P, (first + count) // P):
+                recip_t = sb("recip_t%d" % c, [P, PACK, P], F32)
+                nc.scalar.activation(recip_t[:], work[:, :, c * P : (c + 1) * P], ACT.Sigmoid, scale=-1.0)
+                recip[c] = psum.tile([P, PACK, P], F32, name="recip%d" % c, tag="a%d" % c)
+                for t in range(PACK):
+                    nc.tensor.transpose(recip[c][:, t, :], recip_t[:, t, :], ident[:])
             for t in range(PACK):
                 nc.scalar.activation(
-                    work[:, t, cols], st[t][:].indirect(entries(l2, c * CW, CW)), ACT.Sigmoid, scale=2.0
+                    work[:, t, first : first + count], st[t][:].indirect(entries(l2, first, count)),
+                    ACT.Sigmoid, scale=2.0,
                 )
-            zz = sb("zz%d" % c, [P, 2, CW, PACK], BF16)
-            nc.vector.tensor_tensor(
-                zz[:, 0].rearrange("p (c i) t -> p c t i", i=2), woven(num[:, :, cols]), woven(recip[:]), ALU.mult
-            )
+
+        for first, count in CHUNKS:
+            cols = slice(first, first + count)
+            zz = sb("zz%d" % first, [P, 2, count, PACK], BF16)
+            for c in range(first // P, (first + count) // P):
+                nc.vector.tensor_tensor(
+                    zz[:, 0, c * P - first : (c + 1) * P - first].rearrange("p (c i) t -> p c t i", i=4),
+                    woven(num[:, :, c * P : (c + 1) * P]), woven(recip[c][:]), ALU.mult,
+                )
             for t in range(PACK):
                 nc.vector.tensor_scalar(
                     tanh_g[:, t, cols], work[:, t, cols], 0.5, gn2[:, t : t + 1], ALU.subtract, ALU.mult
                 )
             nc.vector.tensor_tensor(
-                zz[:, 1].rearrange("p (c i) t -> p c t i", i=2),
+                zz[:, 1].rearrange("p (c i) t -> p c t i", i=4),
                 woven(tanh_g[:, :, cols]), woven(st_again[:, :, cols]), ALU.mult,
             )
-            codes = sb("codes%d" % c, [P, 2 * CW], U32)
-            scales = sb("scales%d" % c, [P, 2 * CW], U8)
+            codes = sb("codes%d" % first, [P, 2 * count], U32)
+            scales = sb("scales%d" % first, [P, 2 * count], U8)
             nc.vector.quantize_mx(codes[:].bitcast(FP8X4), scales[:], zz[:].rearrange("p a c t -> p (a c t)"))
             for t in range(PACK):
                 rows = slice(t * P, (t + 1) * P)
                 nc.tensor.matmul_mx(
                     h_acc[t][:, cols], lhsT=w3[:, rows].bitcast(FP8X4), lhsT_scale=w23s[4:, rows],
-                    rhs=codes[:, 0:CW].bitcast(FP8X4), rhs_scale=scales[:, 0:CW], start=True, stop=False,
+                    rhs=codes[:, :count].bitcast(FP8X4), rhs_scale=scales[:, :count], start=True, stop=False,
                 )
                 nc.tensor.matmul_mx(
                     h_acc[t][:, cols], lhsT=w2[:, rows].bitcast(FP8X4), lhsT_scale=w23s[:, rows],
-                    rhs=codes[:, CW:].bitcast(FP8X4), rhs_scale=scales[:, CW:], start=False, stop=True,
+                    rhs=codes[:, count:].bitcast(FP8X4), rhs_scale=scales[:, count:], start=False, stop=True,
                 )
-                if c == S // CW - 1 and t % 2 == 0:
+                if first + count == S and t == 0:
                     nc.vector.tensor_scalar(neg_h[t][:, cols], h_acc[t][:, cols], -1.0, None, ALU.mult)
                 else:
                     nc.scalar.activation(neg_h[t][:, cols], h_acc[t][:, cols], ACT.Copy, scale=-1.0)
-                for first, count in LAST:
-                    if first + count == (c + 1) * CW:
-                        nc.sync.dma_start(neg_h_again[:, t, first : first + count], neg_h[t][:, first : first + count])
+                for start, width in RESULT_CHUNKS[1:]:
+                    if start + width == first + count:
+                        nc.sync.dma_start(neg_h_again[:, t, start : start + width], neg_h[t][:, start : start + width])
 
         out_rows = out_0.rearrange("(p t) j -> p t j", t=PACK)
         out_words = out_1[0].rearrange("p n t -> p (n t)").bitcast(I32)
         o_codes = sb("o_codes", [P, S], U32)
         o_scales = sb("o_scales", [P, S], U8)
-        for first, count in LAST:
+        for first, count in RESULT_CHUNKS:
             cols = slice(first, first + count)
             less4 = sb("less4_%d" % first, [P, PACK, count], F32)
             less5 = sb("less5_%d" % first, [P, PACK, count], F32)
@@ -244,14 +249,20 @@ def tile_picked_joinhoppharmunder_none_po_kernel(
             final = first + count == S
             for t in range(PACK):
                 for dst, lst in ((less4, l4), (less5, l5)):
-                    nc.vector.tensor_tensor(
-                        dst[:, t, :], neg_h[t][:].indirect(entries(lst, first, count)),
-                        neg_h_again[:, t, cols], ALU.subtract,
-                    )
+                    looked_up = neg_h[t][:].indirect(entries(lst, first, count))
+                    if first == 0:
+                        nc.vector.tensor_copy(dst[:, t, :], looked_up)
+                    else:
+                        nc.vector.tensor_tensor(dst[:, t, :], looked_up, neg_h_again[:, t, cols], ALU.subtract)
                 if final and t > 0:
                     nc.vector.tensor_tensor(res[:, t - 1, :], less4[:, t - 1, :], less5[:, t - 1, :], ALU.max)
             if final:
                 nc.vector.tensor_tensor(res[:, PACK - 1, :], less4[:, PACK - 1, :], less5[:, PACK - 1, :], ALU.max)
+            elif first == 0:
+                larger = sb("larger", [P, PACK, count], F32)
+                nc.vector.tensor_tensor(larger[:], less4[:], less5[:], ALU.max)
+                for t in range(PACK):
+                    nc.vector.tensor_tensor(res[:, t, :], larger[:, t, :], h_acc[t][:, cols], ALU.add)
             else:
                 nc.vector.tensor_tensor(res[:], less4[:], less5[:], ALU.max)
             nc.sync.dma_start(out_rows[:, :, cols], res[:])

@@ -74,6 +74,8 @@ def tile_picked_joinhoppharmunder_none_po_kernel(
         nc.vector.memset(w23s_raw[:].bitcast(I32), 0)
         tiny = sb("tiny", [P, 1], F32)
         nc.vector.memset(tiny[:], 2.0**-60)
+        warm = sb("warm", [P, 1], F32)
+        nc.scalar.activation(warm[:], tiny[:], ACT.Ln)
 
         l_offs = load_list("l_offs", offs)
         load_scale_rows_repeated(xs_all, x_scales)

from contextlib import ExitStack

import concourse.mybir as mybir
from concourse.masks import make_identity

K, T, S, N, H = 512, 2048, 512, 512, 512
FLOPS = 3 * 2 * 512 * 512 * 512

F32 = mybir.dt.float32
BF16 = mybir.dt.bfloat16
I32 = mybir.dt.int32
U32 = mybir.dt.uint32
U16 = mybir.dt.uint16
U8 = mybir.dt.uint8
FP8X4 = mybir.dt.float8_e4m3fn_x4
ALU = mybir.AluOpType
ACT = mybir.ActivationFunctionType

P = 128
PACK = 4
CHUNKS = [(0, 256), (256, 128), (384, 128)]
RESULT_CHUNKS = [(0, 128), (128, 256), (384, 128)]


def tile_picked_joinhoppharmunder_none_po_kernel(
    tc, x_words, x_scales, w1_words, w1_scales, gn, gm, w2_words, w2_scales, w3_words, w3_scales,
    offs, n1, n2, n3, n4, n5, out_0, out_1, out_2,
):
    nc = tc.nc
    with ExitStack() as ctx:
        keep = ctx.enter_context(tc.tile_pool(name="keep", bufs=1))
        shared = ctx.enter_context(tc.tile_pool(name="shared", bufs=1))
        psum = ctx.enter_context(tc.psum_pool(name="psum", bufs=1))

        def sb(name, shape, dtype):
            return keep.tile(shape, dtype, name=name, align_bytes=64)

        def load_list(name, src):
            lst = keep.tile([P, S // 16], U16, name=name)
            nc.sync.dma_start(lst[:], src)
            return lst

        def entries(lst, first, count):
            return lst[:, first // 16 : (first + count) // 16]

        def load_words(name, src, cols):
            words = sb(name, [P, cols], I32)
            nc.sync.dma_start(words[:], src[0].rearrange("p n t -> p (n t)").bitcast(I32))
            return words

        def load_scale_rows(plane, src, row0):
            for q in range(4):
                nc.sync.dma_start(
                    plane[32 * q + row0 : 32 * q + row0 + 4, :].bitcast(I32),
                    src[0, 4 * q : 4 * q + 4, :].bitcast(I32),
                )

        def load_scale_rows_repeated(plane, src):
            for q in range(4):
                rows = src[0, 4 * q : 4 * q + 4, :].bitcast(I32)
                nc.sync.dma_start(
                    plane[32 * q : 32 * q + 32, :].bitcast(I32), rows.unsqueeze(0).to_broadcast([8, 4, rows.shape[1]])
                )

        def deal(dst, src, run, first=0, count=PACK):
            nc.vector.tensor_copy(
                dst.rearrange("p (t b i) -> p b t i", t=PACK, i=run)[:, :, first : first + count, :],
                src.rearrange("p (b i t) -> p b t i", t=PACK, i=run)[:, :, first : first + count, :],
            )

        xs_all = sb("xs_all", [P, T], U8)
        w1s_raw = sb("w1s_raw", [P, H], U8)
        w23s_raw = sb("w23s_raw", [P, N], U8)
        nc.vector.memset(w23s_raw[:].bitcast(I32), 0)
        tiny = sb("tiny", [P, 1], F32)
        nc.vector.memset(tiny[:], 2.0**-60)
        warm = sb("warm", [P, 1], F32)
        nc.scalar.activation(warm[:], tiny[:], ACT.Ln)

        l_offs = load_list("l_offs", offs)
        load_scale_rows_repeated(xs_all, x_scales)
        xw_all = load_words("xw_all", x_words, T)
        load_scale_rows_repeated(w1s_raw, w1_scales)
        w1_raw = load_words("w1_raw", w1_words, H)
        l3 = load_list("l3", n3)
        gn_t = sb("gn_t", [P, PACK], F32)
        nc.sync.dma_start(gn_t[:], gn.rearrange("(p t) o -> p (t o)", t=PACK))
        gm_t = sb("gm_t", [P, PACK], F32)
        nc.sync.dma_start(gm_t[:], gm.rearrange("(p t) o -> p (t o)", t=PACK))
        l1 = load_list("l1", n1)
        l2 = load_list("l2", n2)
        w3_raw = load_words("w3_raw", w3_words, N)
        w2_raw = load_words("w2_raw", w2_words, N)
        load_scale_rows(w23s_raw, w2_scales, 0)
        load_scale_rows(w23s_raw, w3_scales, 4)
        l4 = load_list("l4", n4)
        l5 = load_list("l5", n5)

        ident = sb("ident", [P, P], F32)
        make_identity(nc, ident[:])
        gn2 = sb("gn2", [P, PACK], F32)
        nc.scalar.activation(gn2[:], gn_t[:], ACT.Copy, scale=2.0)

        xs = sb("xs", [P, S], U8)
        nc.vector.tensor_copy(xs[:], xs_all[:].indirect(l_offs[:]))
        xw = sb("xw", [P, S], U32)
        w1s = sb("w1s", [P, H], U8)
        w1 = sb("w1", [P, H], I32)
        half = S // 2
        y = [sb("y%d" % t, [P, S], F32) for t in range(PACK)]
        y_again = shared.tile([P, PACK, S], F32, name="y_again", offset=0, align_bytes=64)

        def project(acc, t, cols):
            rows = slice(t * P, (t + 1) * P)
            nc.tensor.matmul_mx(
                acc, lhsT=w1[:, rows].bitcast(FP8X4), lhsT_scale=w1s[:, rows],
                rhs=xw[:, cols].bitcast(FP8X4), rhs_scale=xs[:, cols], start=True, stop=True,
            )

        nc.vector.tensor_copy(xw[:, :half], xw_all[:].bitcast(U32).indirect(entries(l_offs, 0, half)))
        deal(w1s[:], w1s_raw[:], 16)
        deal(w1[:], w1_raw[:], 4, 0, 1)
        early = psum.tile([P, half], F32, name="y_early", tag="b0")
        project(early[:], 0, slice(0, half))
        nc.scalar.copy(y[0][:, :half], early[:])
        nc.vector.tensor_copy(xw[:, half:], xw_all[:].bitcast(U32).indirect(entries(l_offs, half, half)))
        late = psum.tile([P, half], F32, name="y_late", tag="a0")
        project(late[:], 0, slice(half, S))
        deal(w1[:], w1_raw[:], 4, 1, 3)
        nc.vector.tensor_copy(y[0][:, half:], late[:])
        nc.sync.dma_start(y_again[:, 0, :], y[0][:])
        for t in range(1, PACK):
            acc = psum.tile([P, S], F32, name="y_acc%d" % t, tag="a%d" % t)
            project(acc[:], t, slice(0, S))
            nc.scalar.copy(y[t][:], acc[:])
            nc.sync.dma_start(y_again[:, t, :], y[t][:])

        sq_y = sb("sq_y", [P, PACK, S], F32)

        pa = sb("pa", [P, PACK, S], F32)
        sq_pa = sb("sq_pa", [P, PACK, S], F32)
        work = sb("work", [P, PACK, S], F32)
        for t in range(PACK):
            for u in range(2):
                nc.vector.tensor_copy(
                    pa[:, t, u * half : (u + 1) * half], y[t][:].indirect(entries(l3, u * half, half))
                )
            nc.scalar.activation(sq_y[:, t, :], y[t][:], ACT.Square)
            nc.scalar.activation(sq_pa[:, t, :], pa[:, t, :], ACT.Square)
            q_acc = psum.tile([P, S], F32, name="q_acc%d" % t, tag="b%d" % t)
            for k, squares in enumerate((sq_y, sq_pa)):
                for c in range(S // P):
                    cols = slice(c * P, (c + 1) * P)
                    nc.tensor.matmul(
                        q_acc[:, cols], squares[:, t, cols], ident[:],
                        start=(k == 0 and c == 0), stop=(k == 1 and c == S // P - 1), is_transpose=True,
                    )
            nc.scalar.activation(work[:, t, :], q_acc[:], ACT.Ln, bias=tiny[:], scale=2.0)

        st = [sb("st%d" % t, [P, S], F32) for t in range(PACK)]
        st_again = sb("st_again", [P, PACK, S], F32)
        for t in range(PACK):
            for u in range(2):
                cols = slice(u * half, (u + 1) * half)
                nc.vector.tensor_tensor(
                    st[t][:, cols], y[t][:].indirect(entries(l1, u * half, half)), y_again[:, t, cols], ALU.add
                )
            nc.sync.dma_start(st_again[:, t, :], st[t][:])
        gm4 = shared.tile([P, PACK], F32, name="gm4", offset=0, align_bytes=64)
        w23s = shared.tile([P, N], U8, name="w23s", offset=1024, align_bytes=64)
        w2 = shared.tile([P, N], I32, name="w2", offset=2048, align_bytes=64)
        w3 = shared.tile([P, N], I32, name="w3", offset=4096, align_bytes=64)
        nc.vector.tensor_scalar(gm4[:], gm_t[:], 4.0, None, ALU.mult)
        deal(w3[:], w3_raw[:], 4)
        num = sb("num", [P, PACK, S], F32)
        for t in range(PACK):
            nc.vector.scalar_tensor_tensor(
                num[:, t, :], pa[:, t, :], gm4[:, t : t + 1], y[t][:], ALU.mult, ALU.mult
            )
        deal(w2[:], w2_raw[:], 4)
        deal(w23s[:], w23s_raw[:], 16)

        h_acc = [psum.tile([P, S], F32, name="h_acc%d" % t, tag="b%d" % t) for t in range(PACK)]
        neg_h = [sb("neg_h%d" % t, [P, S], F32) for t in range(PACK)]
        neg_h_again = sb("neg_h_again", [P, PACK, S], F32)
        tanh_g = sb("tanh_g", [P, PACK, S], F32)

        def woven(ap):
            return ap.rearrange("p t (c i) -> p c t i", i=4)

        recip = {}
        for first, count in CHUNKS:
            for c in range(first // P, (first + count) // P):
                recip_t = sb("recip_t%d" % c, [P, PACK, P], F32)
                nc.scalar.activation(recip_t[:], work[:, :, c * P : (c + 1) * P], ACT.Sigmoid, scale=-1.0)
                recip[c] = psum.tile([P, PACK, P], F32, name="recip%d" % c, tag="a%d" % c)
                for t in range(PACK):
                    nc.tensor.transpose(recip[c][:, t, :], recip_t[:, t, :], ident[:])
            for t in range(PACK):
                nc.scalar.activation(
                    work[:, t, first : first + count], st[t][:].indirect(entries(l2, first, count)),
                    ACT.Sigmoid, scale=2.0,
                )

        for first, count in CHUNKS:
            cols = slice(first, first + count)
            zz = sb("zz%d" % first, [P, 2, count, PACK], BF16)
            for c in range(first // P, (first + count) // P):
                nc.vector.tensor_tensor(
                    zz[:, 0, c * P - first : (c + 1) * P - first].rearrange("p (c i) t -> p c t i", i=4),
                    woven(num[:, :, c * P : (c + 1) * P]), woven(recip[c][:]), ALU.mult,
                )
            for t in range(PACK):
                nc.vector.tensor_scalar(
                    tanh_g[:, t, cols], work[:, t, cols], 0.5, gn2[:, t : t + 1], ALU.subtract, ALU.mult
                )
            nc.vector.tensor_tensor(
                zz[:, 1].rearrange("p (c i) t -> p c t i", i=4),
                woven(tanh_g[:, :, cols]), woven(st_again[:, :, cols]), ALU.mult,
            )
            codes = sb("codes%d" % first, [P, 2 * count], U32)
            scales = sb("scales%d" % first, [P, 2 * count], U8)
            nc.vector.quantize_mx(codes[:].bitcast(FP8X4), scales[:], zz[:].rearrange("p a c t -> p (a c t)"))
            for t in range(PACK):
                rows = slice(t * P, (t + 1) * P)
                nc.tensor.matmul_mx(
                    h_acc[t][:, cols], lhsT=w3[:, rows].bitcast(FP8X4), lhsT_scale=w23s[4:, rows],
                    rhs=codes[:, :count].bitcast(FP8X4), rhs_scale=scales[:, :count], start=True, stop=False,
                )
                nc.tensor.matmul_mx(
                    h_acc[t][:, cols], lhsT=w2[:, rows].bitcast(FP8X4), lhsT_scale=w23s[:, rows],
                    rhs=codes[:, count:].bitcast(FP8X4), rhs_scale=scales[:, count:], start=False, stop=True,
                )
                if first + count == S and t == 0:
                    nc.vector.tensor_scalar(neg_h[t][:, cols], h_acc[t][:, cols], -1.0, None, ALU.mult)
                else:
                    nc.scalar.activation(neg_h[t][:, cols], h_acc[t][:, cols], ACT.Copy, scale=-1.0)
                for start, width in RESULT_CHUNKS[1:]:
                    if start + width == first + count:
                        nc.sync.dma_start(neg_h_again[:, t, start : start + width], neg_h[t][:, start : start + width])

        out_rows = out_0.rearrange("(p t) j -> p t j", t=PACK)
        out_words = out_1[0].rearrange("p n t -> p (n t)").bitcast(I32)
        o_codes = sb("o_codes", [P, S], U32)
        o_scales = sb("o_scales", [P, S], U8)
        for first, count in RESULT_CHUNKS:
            cols = slice(first, first + count)
            less4 = sb("less4_%d" % first, [P, PACK, count], F32)
            less5 = sb("less5_%d" % first, [P, PACK, count], F32)
            res = sb("res%d" % first, [P, PACK, count], F32)
            final = first + count == S
            for t in range(PACK):
                for dst, lst in ((less4, l4), (less5, l5)):
                    looked_up = neg_h[t][:].indirect(entries(lst, first, count))
                    if first == 0:
                        nc.vector.tensor_copy(dst[:, t, :], looked_up)
                    else:
                        nc.vector.tensor_tensor(dst[:, t, :], looked_up, neg_h_again[:, t, cols], ALU.subtract)
                if final and t > 0:
                    nc.vector.tensor_tensor(res[:, t - 1, :], less4[:, t - 1, :], less5[:, t - 1, :], ALU.max)
            if final:
                nc.vector.tensor_tensor(res[:, PACK - 1, :], less4[:, PACK - 1, :], less5[:, PACK - 1, :], ALU.max)
            elif first == 0:
                larger = sb("larger", [P, PACK, count], F32)
                nc.vector.tensor_tensor(larger[:], less4[:], less5[:], ALU.max)
                for t in range(PACK):
                    nc.vector.tensor_tensor(res[:, t, :], larger[:, t, :], h_acc[t][:, cols], ALU.add)
            else:
                nc.vector.tensor_tensor(res[:], less4[:], less5[:], ALU.max)
            nc.sync.dma_start(out_rows[:, :, cols], res[:])
            rounded = sb("rounded%d" % first, [P, count, PACK], BF16)
            copy = nc.vector.tensor_copy if first + count == S else nc.scalar.copy
            copy(
                rounded[:].rearrange("p (c i) t -> p c t i", i=4),
                res[:].rearrange("p t (c i) -> p c t i", i=4),
            )
            nc.vector.quantize_mx(
                o_codes[:, cols].bitcast(FP8X4), o_scales[:, cols], rounded[:].rearrange("p c t -> p (c t)")
            )
            nc.sync.dma_start(out_words[:, cols], o_codes[:, cols].bitcast(I32))
        for q in range(4):
            queue = nc.sync if q % 2 else nc.scalar
            queue.dma_start(out_2[0, 4 * q : 4 * q + 4, :].bitcast(I32), o_scales[32 * q : 32 * q + 4, :].bitcast(I32))
